import numpy as np, ml_dtypes
CORES = [33,38,57,62,81,86,161,166,185,190,209,214]
N = 12
TK = 128
WID = [80,32,64,112,128,80,128,16,16,128,128,112]
def setup_inputs(rng):
    return {"x": rng.standard_normal((N, 128, TK), dtype=np.float32).astype(ml_dtypes.bfloat16), "w": rng.standard_normal((N, 128, 128), dtype=np.float32).astype(ml_dtypes.bfloat16)}
def setup_inputs_big(rng):
    d = setup_inputs(rng)
    for k in ("x", "w"): d[k] = (d[k].astype(np.float32) * 1024.0).astype(d[k].dtype)
    return d
def setup_inputs_small(rng):
    d = setup_inputs(rng)
    for k in ("x", "w"): d[k] = (d[k].astype(np.float32) * (1 / 1024.0)).astype(d[k].dtype)
    return d
def setup_inputs_apart(rng):
    d = setup_inputs(rng)
    f = (10.0 ** rng.permutation(np.linspace(-1.5, 1.5, N))).astype(np.float32).reshape(N, 1, 1)
    for k in ("x", "w"): d[k] = (d[k].astype(np.float32) * f).astype(d[k].dtype)
    return d
def setup_inputs_neg(rng):
    d = setup_inputs(rng)
    d["x"] = (np.abs(d["x"].astype(np.float32)) * 1048576.0).astype(d["x"].dtype); d["w"] = (-np.abs(d["w"].astype(np.float32))).astype(d["w"].dtype)
    return d
def whole(x, w):
    X, W = x.astype(np.float64), w.astype(np.float64)
    y = np.stack([np.max([W[j].T @ X[r] for j in range(N)], axis=0) for r in range(N)])
    return {"y": y.astype(ml_dtypes.bfloat16)}
def reference(x, w):
    o = whole(x, w)["y"].copy()
    for r in range(N):
        o[r][:, WID[r]:] = np.nan
    return {"y": o}

@@ -1,0 +1,184 @@
+from concourse.bass import DstId, RemoteDMATransfer
+from concourse.mybir import AluOpType
+
+N = 12
+D = 128
+BOTH, OWN = 0, 1
+NBANK = 8
+
+SCRATCH = {
+    "land": ("dram", [N, D, D], "bfloat16"),
+    "wsb": ("sbuf", [D, N * D], "bfloat16"),
+    "xx": ("sbuf", [D, 2 * D], "bfloat16"),
+    "acc": ("sbuf", [D, 2 * D], "bfloat16"),
+    "prec": ("sbuf", [D, D], "bfloat16"),
+    "yb": ("sbuf", [D, D], "bfloat16"),
+}
+for _k in range(NBANK):
+    SCRATCH["ps%d" % _k] = ("psum", [D, 512], "float32")
+
+SEMAPHORES = ["ldd", "lds", "ldx", "xa", "pa", "pv", "vv", "fv", "st", "loc"]
+SEMAPHORES += ["a%d" % _j for _j in range(N)] + ["s%d" % _j for _j in range(N)] + ["m%d" % _j for _j in range(N)]
+
+
+def _pop(m):
+    return bin(m).count("1")
+
+
+def _common(topo, src, dsts):
+    bits = -1
+    for d in dsts:
+        bits &= topo.mask(src, d)
+    n = 1
+    while n * 2 <= _pop(bits):
+        n *= 2
+    m, b = 0, 0
+    while _pop(m) < n:
+        if (bits >> b) & 1:
+            m |= 1 << b
+        b += 1
+    return m
+
+
+def _plan(cores, topo):
+    n = len(cores)
+    place = [(topo.host(c), topo.chip(c)) for c in cores]
+    chips = sorted(set(place))
+    members = dict((ch, [r for r in range(n) if place[r] == ch]) for ch in chips)
+    partner = [[q for q in members[place[r]] if q != r][0] for r in range(n)]
+    target = {}
+    for ch in chips:
+        a, b = members[ch]
+        off = [j for j in range(n) if place[j] != ch]
+        early = [j for j in off if topo.may_write(cores[j], cores[a])]
+        early.sort(key=lambda j: (topo.die(cores[j]) != topo.die(cores[a]), j))
+        half = (len(early) + 1) // 2
+        for i, j in enumerate(early):
+            target[(j, ch)] = ([a if i < half else b], BOTH)
+        for j in off:
+            if j not in early:
+                target[(j, ch)] = ([a, b], OWN)
+    first = [[] for _ in range(n)]
+    second = [[] for _ in range(n)]
+    mode = {}
+    for j in range(n):
+        i0 = chips.index(place[j])
+        for s in range(1, len(chips)):
+            ch = chips[(i0 + s) % len(chips)]
+            ranks, md = target[(j, ch)]
+            (first if md == BOTH else second)[j].extend(ranks)
+            for r in ranks:
+                mode[(j, r)] = md
+        if second[j]:
+            first[j].insert(0, partner[j])
+    narr = {}
+    pos = {}
+    for j in range(n):
+        m1 = _common(topo, cores[j], [cores[d] for d in first[j]])
+        for i, d in enumerate(first[j]):
+            narr[(j, d)] = _pop(m1)
+            pos[(j, d)] = i
+        if second[j]:
+            m2 = _common(topo, cores[partner[j]], [cores[d] for d in second[j]])
+            for i, d in enumerate(second[j]):
+                narr[(j, d)] = _pop(m2)
+                pos[(j, d)] = 100 + i
+    consume = []
+    for r in range(n):
+        got = [j for j in range(n) if (j, r) in mode]
+        got.sort(key=lambda j: (mode[(j, r)], pos[(j, r)], j))
+        consume.append([(r, BOTH)] + [(j, mode[(j, r)]) for j in got])
+    return dict(partner=partner, first=first, second=second, narr=narr, consume=consume)
+
+
+def rank_program(g, core, T, topo):
+    me = T.rank_of(core)
+    if me is None:
+        return
+    cores = list(T.cores)
+    wid = T.tables["WID"]
+    P = _plan(cores, topo)
+    S = T.sem
+    pa = P["partner"][me]
+    cons = P["consume"][me]
+    narr = P["narr"]
+    Wo, Wp = wid[me], wid[pa]
+    Wt = Wo + Wp
+
+    def slot(j):
+        return T.wsb[:, j * D:(j + 1) * D]
+
+    g.sync.dma_start(T.land[me], T.w[:]).then_inc(S.ldd, 16)
+    g.scalar.dma_start(T.xx[:, Wp:Wt], T.x[:, 0:Wo]).then_inc(S.ldx, 16)
+    g.sync.dma_start(slot(me), T.w[:]).then_inc(S.lds, 16)
+
+    sent = [0]
+
+    def fan(j, dests):
+        m = _common(topo, core, [cores[d] for d in dests])
+        ids = []
+        for d in dests:
+            rid, pid = topo.addr(cores[d], core)
+            ids.append(DstId(rid=rid, pnc=pid))
+        g.remote_dma_fused([RemoteDMATransfer(dst_ids=ids, dma_engine_mask=m, remote_sem=S["a%d" % j],
+                                              srcs=[T.land[j]], dsts=[T.land[j] for _ in dests])], local_sem=S.loc)
+        sent[0] += _pop(m)
+        return m
+
+    g.wait_ge(S.ldd, 16)
+    warm = fan(me, P["first"][me])
+    prid, ppid = topo.addr(cores[pa], core)
+    mon = warm & topo.mask(core, cores[pa])
+    g.wait_ge(S.ldx, 16)
+    g.remote_dma(out_ap=T.xx[:, 0:Wo], in_ap=T.xx[:, Wp:Wt], remote_sem=S.xa, local_sem=S.loc,
+                 pid=ppid, routing_id=prid, dma_engine_mask=mon)
+    sent[0] += _pop(mon)
+    if P["second"][pa]:
+        g.wait_ge(S["a%d" % pa], narr[(pa, me)])
+        fan(pa, P["second"][pa])
+
+    qs = [g.sync, g.scalar]
+    for i, (j, md) in enumerate(cons[1:]):
+        q = qs[i % 2]
+        q.wait_ge(S["a%d" % j], narr[(j, me)])
+        q.dma_start(slot(j), T.land[j]).then_inc(S["s%d" % j], 16)
+
+    pmon = _pop(_common(topo, cores[pa], [cores[d] for d in P["first"][pa]]) & topo.mask(cores[pa], core))
+    last_both = max(k for k, (j, md) in enumerate(cons) if md == BOTH)
+    nv = 0
+    for k, (j, md) in enumerate(cons):
+        ps = T["ps%d" % k]
+        if k == 0:
+            g.tensor.wait_ge(S.lds, 16)
+            g.tensor.wait_ge(S.ldx, 16)
+            g.tensor.wait_ge(S.xa, pmon)
+        else:
+            g.tensor.wait_ge(S["s%d" % j], 16)
+        c0 = 0 if md == BOTH else Wp
+        g.tensor.matmul(ps[:, c0:Wt], slot(j), T.xx[:, c0:Wt], start=True, stop=True).then_inc(S["m%d" % j], 1)
+        g.vector.wait_ge(S["m%d" % j], 1)
+        if nv:
+            g.vector.wait_ge(S.vv, nv)
+        parts = [(c0, Wt, S.vv)]
+        if k == last_both:
+            parts = [(0, Wp, S.pv), (Wp, Wt, S.vv)]
+        for (a, b, sem) in parts:
+            if k == 0:
+                g.vector.tensor_copy(T.acc[:, a:b], ps[:, a:b]).then_inc(sem, 1)
+            else:
+                g.vector.tensor_tensor(T.acc[:, a:b], T.acc[:, a:b], ps[:, a:b], AluOpType.max).then_inc(sem, 1)
+        nv += 1
+
+    g.wait_ge(S.pv, 1)
+    g.remote_dma(out_ap=T.prec[:, 0:Wp], in_ap=T.acc[:, 0:Wp], remote_sem=S.pa, local_sem=S.loc,
+                 pid=ppid, routing_id=prid, dma_engine_mask=mon)
+    sent[0] += _pop(mon)
+
+    g.vector.wait_ge(S.vv, nv)
+    g.vector.wait_ge(S.pa, pmon)
+    g.vector.tensor_tensor(T.yb[:, 0:Wo], T.acc[:, Wp:Wt], T.prec[:, 0:Wo], AluOpType.max).then_inc(S.fv, 1)
+    g.sync.wait_ge(S.fv, 1)
+    g.sync.dma_start(T.y[:, 0:Wo], T.yb[:, 0:Wo]).then_inc(S.st, 16)
+
+    g.wait_ge(S.loc, sent[0])
+    g.wait_ge(S.st, 16)

@@ -3,8 +3,9 @@ from concourse.mybir import AluOpType
 
 N = 12
 D = 128
-BOTH, OWN = 0, 1
+NCORES = 256
 NBANK = 8
+NHELP = 3
 
 SCRATCH = {
     "land": ("dram", [N, D, D], "bfloat16"),
@@ -17,7 +18,7 @@ SCRATCH = {
 for _k in range(NBANK):
     SCRATCH["ps%d" % _k] = ("psum", [D, 512], "float32")
 
-SEMAPHORES = ["ldd", "lds", "ldx", "xa", "pa", "pv", "vv", "fv", "st", "loc"]
+SEMAPHORES = ["ldd", "lds", "ldx", "xa", "pa", "pv", "vv", "fv", "st", "loc", "mz"]
 SEMAPHORES += ["a%d" % _j for _j in range(N)] + ["s%d" % _j for _j in range(N)] + ["m%d" % _j for _j in range(N)]
 
 
@@ -25,10 +26,7 @@ def _pop(m):
     return bin(m).count("1")
 
 
-def _common(topo, src, dsts):
-    bits = -1
-    for d in dsts:
-        bits &= topo.mask(src, d)
+def _pick(bits):
     n = 1
     while n * 2 <= _pop(bits):
         n *= 2
@@ -40,142 +38,164 @@ def _common(topo, src, dsts):
     return m
 
 
+def _shared(topo, src, dsts):
+    bits = -1
+    for d in dsts:
+        bits &= topo.mask(src, d)
+    return bits
+
+
 def _plan(cores, topo):
     n = len(cores)
     place = [(topo.host(c), topo.chip(c)) for c in cores]
     chips = sorted(set(place))
     members = dict((ch, [r for r in range(n) if place[r] == ch]) for ch in chips)
     partner = [[q for q in members[place[r]] if q != r][0] for r in range(n)]
-    target = {}
-    for ch in chips:
-        a, b = members[ch]
-        off = [j for j in range(n) if place[j] != ch]
-        early = [j for j in off if topo.may_write(cores[j], cores[a])]
-        early.sort(key=lambda j: (topo.die(cores[j]) != topo.die(cores[a]), j))
-        half = (len(early) + 1) // 2
-        for i, j in enumerate(early):
-            target[(j, ch)] = ([a if i < half else b], BOTH)
-        for j in off:
-            if j not in early:
-                target[(j, ch)] = ([a, b], OWN)
-    first = [[] for _ in range(n)]
-    second = [[] for _ in range(n)]
-    mode = {}
-    for j in range(n):
-        i0 = chips.index(place[j])
-        for s in range(1, len(chips)):
-            ch = chips[(i0 + s) % len(chips)]
-            ranks, md = target[(j, ch)]
-            (first if md == BOTH else second)[j].extend(ranks)
-            for r in ranks:
-                mode[(j, r)] = md
-        if second[j]:
-            first[j].insert(0, partner[j])
-    narr = {}
+
+    def receiver(j, ch):
+        same = [r for r in members[ch] if topo.die(cores[r]) == topo.die(cores[j])]
+        return (same or members[ch])[0]
+
+    direct = [[] for _ in range(n)]
+    hand = [[] for _ in range(n)]
+    relay = {}
     pos = {}
     for j in range(n):
-        m1 = _common(topo, cores[j], [cores[d] for d in first[j]])
-        for i, d in enumerate(first[j]):
-            narr[(j, d)] = _pop(m1)
-            pos[(j, d)] = i
-        if second[j]:
-            m2 = _common(topo, cores[partner[j]], [cores[d] for d in second[j]])
-            for i, d in enumerate(second[j]):
-                narr[(j, d)] = _pop(m2)
-                pos[(j, d)] = 100 + i
+        i0 = chips.index(place[j])
+        far = []
+        for s in range(1, len(chips)):
+            r = receiver(j, chips[(i0 + s) % len(chips)])
+            if topo.may_write(cores[j], cores[r]):
+                pos[(j, r)] = len(direct[j])
+                direct[j].append(r)
+            else:
+                far.append(r)
+        if far:
+            idle = [c for c in range(NCORES) if c not in cores and (topo.host(c), topo.chip(c)) == place[j]
+                    and all(topo.may_write(c, cores[r]) for r in far)]
+            mine = [c for c in idle if topo.die(c) == topo.die(cores[j])]
+            other = [c for c in idle if topo.die(c) != topo.die(cores[j])]
+            hand[j] = (mine + other)[:min(NHELP, len(far))]
+            for i, h in enumerate(hand[j]):
+                relay[h] = (j, far[i::len(hand[j])])
+                for t, r in enumerate(relay[h][1]):
+                    pos[(j, r)] = 100 + 10 * t + i
+    masks = []
+    for j in range(n):
+        fan = _pick(_shared(topo, cores[j], [cores[r] for r in direct[j]]))
+        near = _shared(topo, cores[j], [cores[partner[j]]] + hand[j])
+        only = _pick(near & ~fan) if near & ~fan else _pick(near & fan)
+        masks.append((fan, only, _pick(near & (fan | only))))
+    narr = {}
+    late = set()
+    for j in range(n):
+        for r in direct[j]:
+            narr[(j, r)] = _pop(masks[j][0])
+    for h, (j, rs) in relay.items():
+        for r in rs:
+            narr[(j, r)] = _pop(_pick(_shared(topo, h, [cores[q] for q in rs])))
+            late.add((j, r))
     consume = []
     for r in range(n):
-        got = [j for j in range(n) if (j, r) in mode]
-        got.sort(key=lambda j: (mode[(j, r)], pos[(j, r)], j))
-        consume.append([(r, BOTH)] + [(j, mode[(j, r)]) for j in got])
-    return dict(partner=partner, first=first, second=second, narr=narr, consume=consume)
+        got = sorted([j for j in range(n) if (j, r) in pos], key=lambda j: (pos[(j, r)], j))
+        consume.append([r] + got)
+    return dict(partner=partner, direct=direct, hand=hand, relay=relay, masks=masks, narr=narr, late=late, consume=consume)
 
 
 def rank_program(g, core, T, topo):
-    me = T.rank_of(core)
-    if me is None:
-        return
     cores = list(T.cores)
-    wid = T.tables["WID"]
     P = _plan(cores, topo)
     S = T.sem
-    pa = P["partner"][me]
-    cons = P["consume"][me]
-    narr = P["narr"]
-    Wo, Wp = wid[me], wid[pa]
-    Wt = Wo + Wp
+    me = T.rank_of(core)
+    sent = [0]
 
     def slot(j):
         return T.wsb[:, j * D:(j + 1) * D]
+
+    def fan(j, dst_cores, m, into_sbuf):
+        ids = []
+        for d in dst_cores:
+            rid, pid = topo.addr(d, core)
+            ids.append(DstId(rid=rid, pnc=pid))
+        out = slot(j) if into_sbuf else T.land[j]
+        g.remote_dma_fused([RemoteDMATransfer(dst_ids=ids, dma_engine_mask=m, remote_sem=S["a%d" % j],
+                                              srcs=[T.land[j]], dsts=[out for _ in dst_cores])], local_sem=S.loc)
+        sent[0] += _pop(m)
+
+    if me is None:
+        if core in P["relay"]:
+            j, rs = P["relay"][core]
+            dst = [cores[r] for r in rs]
+            g.wait_ge(S["a%d" % j], _pop(P["masks"][j][1]))
+            fan(j, dst, _pick(_shared(topo, core, dst)), True)
+            g.wait_ge(S.loc, sent[0])
+        return
+
+    wid = T.tables["WID"]
+    pa = P["partner"][me]
+    cons = P["consume"][me]
+    narr = P["narr"]
+    late = P["late"]
+    mfan, monly, mall = P["masks"][me]
+    Wo, Wp = wid[me], wid[pa]
+    Wt = Wo + Wp
 
     g.sync.dma_start(T.land[me], T.w[:]).then_inc(S.ldd, 16)
     g.scalar.dma_start(T.xx[:, Wp:Wt], T.x[:, 0:Wo]).then_inc(S.ldx, 16)
     g.sync.dma_start(slot(me), T.w[:]).then_inc(S.lds, 16)
 
-    sent = [0]
-
-    def fan(j, dests):
-        m = _common(topo, core, [cores[d] for d in dests])
-        ids = []
-        for d in dests:
-            rid, pid = topo.addr(cores[d], core)
-            ids.append(DstId(rid=rid, pnc=pid))
-        g.remote_dma_fused([RemoteDMATransfer(dst_ids=ids, dma_engine_mask=m, remote_sem=S["a%d" % j],
-                                              srcs=[T.land[j]], dsts=[T.land[j] for _ in dests])], local_sem=S.loc)
-        sent[0] += _pop(m)
-        return m
-
     g.wait_ge(S.ldd, 16)
-    warm = fan(me, P["first"][me])
+    if P["hand"][me]:
+        fan(me, P["hand"][me], monly, False)
+    fan(me, [cores[r] for r in P["direct"][me]], mfan, False)
     prid, ppid = topo.addr(cores[pa], core)
-    mon = warm & topo.mask(core, cores[pa])
     g.wait_ge(S.ldx, 16)
     g.remote_dma(out_ap=T.xx[:, 0:Wo], in_ap=T.xx[:, Wp:Wt], remote_sem=S.xa, local_sem=S.loc,
-                 pid=ppid, routing_id=prid, dma_engine_mask=mon)
-    sent[0] += _pop(mon)
-    if P["second"][pa]:
-        g.wait_ge(S["a%d" % pa], narr[(pa, me)])
-        fan(pa, P["second"][pa])
+                 pid=ppid, routing_id=prid, dma_engine_mask=monly)
+    sent[0] += _pop(monly)
 
     qs = [g.sync, g.scalar]
-    for i, (j, md) in enumerate(cons[1:]):
+    for i, j in enumerate([j for j in cons[1:] if (j, me) not in late]):
         q = qs[i % 2]
         q.wait_ge(S["a%d" % j], narr[(j, me)])
         q.dma_start(slot(j), T.land[j]).then_inc(S["s%d" % j], 16)
 
-    pmon = _pop(_common(topo, cores[pa], [cores[d] for d in P["first"][pa]]) & topo.mask(cores[pa], core))
-    last_both = max(k for k, (j, md) in enumerate(cons) if md == BOTH)
-    nv = 0
-    for k, (j, md) in enumerate(cons):
+    last = len(cons) - 1
+    for k, j in enumerate(cons):
         ps = T["ps%d" % k]
         if k == 0:
             g.tensor.wait_ge(S.lds, 16)
             g.tensor.wait_ge(S.ldx, 16)
-            g.tensor.wait_ge(S.xa, pmon)
+            g.tensor.wait_ge(S.xa, _pop(P["masks"][pa][1]))
+        elif (j, me) in late:
+            g.tensor.wait_ge(S["a%d" % j], narr[(j, me)])
         else:
             g.tensor.wait_ge(S["s%d" % j], 16)
-        c0 = 0 if md == BOTH else Wp
-        g.tensor.matmul(ps[:, c0:Wt], slot(j), T.xx[:, c0:Wt], start=True, stop=True).then_inc(S["m%d" % j], 1)
-        g.vector.wait_ge(S["m%d" % j], 1)
-        if nv:
-            g.vector.wait_ge(S.vv, nv)
-        parts = [(c0, Wt, S.vv)]
-        if k == last_both:
-            parts = [(0, Wp, S.pv), (Wp, Wt, S.vv)]
-        for (a, b, sem) in parts:
+        if k < last:
+            g.tensor.matmul(ps[:, 0:Wt], slot(j), T.xx[:, 0:Wt], start=True, stop=True).then_inc(S["m%d" % j], 1)
+            g.vector.wait_ge(S["m%d" % j], 1)
             if k == 0:
-                g.vector.tensor_copy(T.acc[:, a:b], ps[:, a:b]).then_inc(sem, 1)
+                g.vector.tensor_copy(T.acc[:, 0:Wt], ps[:, 0:Wt]).then_inc(S.vv, 1)
             else:
-                g.vector.tensor_tensor(T.acc[:, a:b], T.acc[:, a:b], ps[:, a:b], AluOpType.max).then_inc(sem, 1)
-        nv += 1
+                g.vector.wait_ge(S.vv, k)
+                g.vector.tensor_tensor(T.acc[:, 0:Wt], T.acc[:, 0:Wt], ps[:, 0:Wt], AluOpType.max).then_inc(S.vv, 1)
+        else:
+            ps2 = T["ps%d" % (k + 1)]
+            g.tensor.matmul(ps[:, 0:Wp], slot(j), T.xx[:, 0:Wp], start=True, stop=True).then_inc(S["m%d" % j], 1)
+            g.tensor.matmul(ps2[:, Wp:Wt], slot(j), T.xx[:, Wp:Wt], start=True, stop=True).then_inc(S.mz, 1)
+            g.vector.wait_ge(S["m%d" % j], 1)
+            g.vector.wait_ge(S.vv, k)
+            g.vector.tensor_tensor(T.acc[:, 0:Wp], T.acc[:, 0:Wp], ps[:, 0:Wp], AluOpType.max).then_inc(S.pv, 1)
+            g.vector.wait_ge(S.mz, 1)
+            g.vector.tensor_tensor(T.acc[:, Wp:Wt], T.acc[:, Wp:Wt], ps2[:, Wp:Wt], AluOpType.max).then_inc(S.vv, 1)
 
     g.wait_ge(S.pv, 1)
     g.remote_dma(out_ap=T.prec[:, 0:Wp], in_ap=T.acc[:, 0:Wp], remote_sem=S.pa, local_sem=S.loc,
-                 pid=ppid, routing_id=prid, dma_engine_mask=mon)
-    sent[0] += _pop(mon)
+                 pid=ppid, routing_id=prid, dma_engine_mask=mall)
+    sent[0] += _pop(mall)
 
-    g.vector.wait_ge(S.vv, nv)
-    g.vector.wait_ge(S.pa, pmon)
+    g.vector.wait_ge(S.vv, last + 1)
+    g.vector.wait_ge(S.pa, _pop(P["masks"][pa][2]))
     g.vector.tensor_tensor(T.yb[:, 0:Wo], T.acc[:, Wp:Wt], T.prec[:, 0:Wo], AluOpType.max).then_inc(S.fv, 1)
     g.sync.wait_ge(S.fv, 1)
     g.sync.dma_start(T.y[:, 0:Wo], T.yb[:, 0:Wo]).then_inc(S.st, 16)

from concourse.bass import DstId, RemoteDMATransfer
from concourse.mybir import AluOpType

N = 12
D = 128
NCORES = 256
NBANK = 8
NHELP = 3

SCRATCH = {
    "land": ("dram", [N, D, D], "bfloat16"),
    "wsb": ("sbuf", [D, N * D], "bfloat16"),
    "xx": ("sbuf", [D, 2 * D], "bfloat16"),
    "acc": ("sbuf", [D, 2 * D], "bfloat16"),
    "prec": ("sbuf", [D, D], "bfloat16"),
    "yb": ("sbuf", [D, D], "bfloat16"),
}
for _k in range(NBANK):
    SCRATCH["ps%d" % _k] = ("psum", [D, 512], "float32")

SEMAPHORES = ["ldd", "lds", "ldx", "xa", "pa", "pv", "vv", "fv", "st", "loc", "mz"]
SEMAPHORES += ["a%d" % _j for _j in range(N)] + ["s%d" % _j for _j in range(N)] + ["m%d" % _j for _j in range(N)]


def _pop(m):
    return bin(m).count("1")


def _pick(bits):
    n = 1
    while n * 2 <= _pop(bits):
        n *= 2
    m, b = 0, 0
    while _pop(m) < n:
        if (bits >> b) & 1:
            m |= 1 << b
        b += 1
    return m


def _shared(topo, src, dsts):
    bits = -1
    for d in dsts:
        bits &= topo.mask(src, d)
    return bits


def _plan(cores, topo):
    n = len(cores)
    place = [(topo.host(c), topo.chip(c)) for c in cores]
    chips = sorted(set(place))
    members = dict((ch, [r for r in range(n) if place[r] == ch]) for ch in chips)
    partner = [[q for q in members[place[r]] if q != r][0] for r in range(n)]

    def receiver(j, ch):
        same = [r for r in members[ch] if topo.die(cores[r]) == topo.die(cores[j])]
        return (same or members[ch])[0]

    direct = [[] for _ in range(n)]
    hand = [[] for _ in range(n)]
    relay = {}
    pos = {}
    for j in range(n):
        i0 = chips.index(place[j])
        far = []
        for s in range(1, len(chips)):
            r = receiver(j, chips[(i0 + s) % len(chips)])
            if topo.may_write(cores[j], cores[r]):
                pos[(j, r)] = len(direct[j])
                direct[j].append(r)
            else:
                far.append(r)
        if far:
            idle = [c for c in range(NCORES) if c not in cores and (topo.host(c), topo.chip(c)) == place[j]
                    and all(topo.may_write(c, cores[r]) for r in far)]
            mine = [c for c in idle if topo.die(c) == topo.die(cores[j])]
            other = [c for c in idle if topo.die(c) != topo.die(cores[j])]
            hand[j] = (mine + other)[:min(NHELP, len(far))]
            for i, h in enumerate(hand[j]):
                relay[h] = (j, far[i::len(hand[j])])
                for t, r in enumerate(relay[h][1]):
                    pos[(j, r)] = 100 + 10 * t + i
    masks = []
    for j in range(n):
        fan = _pick(_shared(topo, cores[j], [cores[r] for r in direct[j]]))
        near = _shared(topo, cores[j], [cores[partner[j]]] + hand[j])
        only = _pick(near & ~fan) if near & ~fan else _pick(near & fan)
        masks.append((fan, only, _pick(near & (fan | only))))
    narr = {}
    late = set()
    for j in range(n):
        for r in direct[j]:
            narr[(j, r)] = _pop(masks[j][0])
    for h, (j, rs) in relay.items():
        for r in rs:
            narr[(j, r)] = _pop(_pick(_shared(topo, h, [cores[q] for q in rs])))
            late.add((j, r))
    consume = []
    for r in range(n):
        got = sorted([j for j in range(n) if (j, r) in pos], key=lambda j: (pos[(j, r)], j))
        consume.append([r] + got)
    return dict(partner=partner, direct=direct, hand=hand, relay=relay, masks=masks, narr=narr, late=late, consume=consume)


def rank_program(g, core, T, topo):
    cores = list(T.cores)
    P = _plan(cores, topo)
    S = T.sem
    me = T.rank_of(core)
    sent = [0]

    def slot(j):
        return T.wsb[:, j * D:(j + 1) * D]

    def fan(j, dst_cores, m, into_sbuf):
        ids = []
        for d in dst_cores:
            rid, pid = topo.addr(d, core)
            ids.append(DstId(rid=rid, pnc=pid))
        out = slot(j) if into_sbuf else T.land[j]
        g.remote_dma_fused([RemoteDMATransfer(dst_ids=ids, dma_engine_mask=m, remote_sem=S["a%d" % j],
                                              srcs=[T.land[j]], dsts=[out for _ in dst_cores])], local_sem=S.loc)
        sent[0] += _pop(m)

    if me is None:
        if core in P["relay"]:
            j, rs = P["relay"][core]
            dst = [cores[r] for r in rs]
            g.wait_ge(S["a%d" % j], _pop(P["masks"][j][1]))
            fan(j, dst, _pick(_shared(topo, core, dst)), True)
            g.wait_ge(S.loc, sent[0])
        return

    wid = T.tables["WID"]
    pa = P["partner"][me]
    cons = P["consume"][me]
    narr = P["narr"]
    late = P["late"]
    mfan, monly, mall = P["masks"][me]
    Wo, Wp = wid[me], wid[pa]
    Wt = Wo + Wp

    g.sync.dma_start(T.land[me], T.w[:]).then_inc(S.ldd, 16)
    g.scalar.dma_start(T.xx[:, Wp:Wt], T.x[:, 0:Wo]).then_inc(S.ldx, 16)
    g.sync.dma_start(slot(me), T.w[:]).then_inc(S.lds, 16)

    g.wait_ge(S.ldd, 16)
    if P["hand"][me]:
        fan(me, P["hand"][me], monly, False)
    fan(me, [cores[r] for r in P["direct"][me]], mfan, False)
    prid, ppid = topo.addr(cores[pa], core)
    g.wait_ge(S.ldx, 16)
    g.remote_dma(out_ap=T.xx[:, 0:Wo], in_ap=T.xx[:, Wp:Wt], remote_sem=S.xa, local_sem=S.loc,
                 pid=ppid, routing_id=prid, dma_engine_mask=monly)
    sent[0] += _pop(monly)

    qs = [g.sync, g.scalar]
    for i, j in enumerate([j for j in cons[1:] if (j, me) not in late]):
        q = qs[i % 2]
        q.wait_ge(S["a%d" % j], narr[(j, me)])
        q.dma_start(slot(j), T.land[j]).then_inc(S["s%d" % j], 16)

    last = len(cons) - 1
    for k, j in enumerate(cons):
        ps = T["ps%d" % k]
        if k == 0:
            g.tensor.wait_ge(S.lds, 16)
            g.tensor.wait_ge(S.ldx, 16)
            g.tensor.wait_ge(S.xa, _pop(P["masks"][pa][1]))
        elif (j, me) in late:
            g.tensor.wait_ge(S["a%d" % j], narr[(j, me)])
        else:
            g.tensor.wait_ge(S["s%d" % j], 16)
        if k < last:
            g.tensor.matmul(ps[:, 0:Wt], slot(j), T.xx[:, 0:Wt], start=True, stop=True).then_inc(S["m%d" % j], 1)
            g.vector.wait_ge(S["m%d" % j], 1)
            if k == 0:
                g.vector.tensor_copy(T.acc[:, 0:Wt], ps[:, 0:Wt]).then_inc(S.vv, 1)
            else:
                g.vector.wait_ge(S.vv, k)
                g.vector.tensor_tensor(T.acc[:, 0:Wt], T.acc[:, 0:Wt], ps[:, 0:Wt], AluOpType.max).then_inc(S.vv, 1)
        else:
            ps2 = T["ps%d" % (k + 1)]
            g.tensor.matmul(ps[:, 0:Wp], slot(j), T.xx[:, 0:Wp], start=True, stop=True).then_inc(S["m%d" % j], 1)
            g.tensor.matmul(ps2[:, Wp:Wt], slot(j), T.xx[:, Wp:Wt], start=True, stop=True).then_inc(S.mz, 1)
            g.vector.wait_ge(S["m%d" % j], 1)
            g.vector.wait_ge(S.vv, k)
            g.vector.tensor_tensor(T.acc[:, 0:Wp], T.acc[:, 0:Wp], ps[:, 0:Wp], AluOpType.max).then_inc(S.pv, 1)
            g.vector.wait_ge(S.mz, 1)
            g.vector.tensor_tensor(T.acc[:, Wp:Wt], T.acc[:, Wp:Wt], ps2[:, Wp:Wt], AluOpType.max).then_inc(S.vv, 1)

    g.wait_ge(S.pv, 1)
    g.remote_dma(out_ap=T.prec[:, 0:Wp], in_ap=T.acc[:, 0:Wp], remote_sem=S.pa, local_sem=S.loc,
                 pid=ppid, routing_id=prid, dma_engine_mask=mall)
    sent[0] += _pop(mall)

    g.vector.wait_ge(S.vv, last + 1)
    g.vector.wait_ge(S.pa, _pop(P["masks"][pa][2]))
    g.vector.tensor_tensor(T.yb[:, 0:Wo], T.acc[:, Wp:Wt], T.prec[:, 0:Wo], AluOpType.max).then_inc(S.fv, 1)
    g.sync.wait_ge(S.fv, 1)
    g.sync.dma_start(T.y[:, 0:Wo], T.yb[:, 0:Wo]).then_inc(S.st, 16)

    g.wait_ge(S.loc, sent[0])
    g.wait_ge(S.st, 16)
